import numpy as np
import ml_dtypes


def mxq(x, axis, fmt="e4m3"):
    dtype, down = {"e4m3": (ml_dtypes.float8_e4m3fn, 7), "e5m2": (ml_dtypes.float8_e5m2, 14)}[fmt]
    v = np.moveaxis(np.asarray(x, np.float32).astype(ml_dtypes.bfloat16).astype(np.float64), axis, -1)
    blocks = v.reshape(v.shape[:-1] + (-1, 32))
    amax = np.abs(blocks).max(-1, keepdims=True)
    byte = np.maximum(np.where(amax > 0, np.frexp(amax)[1] - 1 + 127, 0) - down, 1)
    scale = np.exp2(byte - 127.0)
    codes = (blocks / scale).astype(np.float32).astype(dtype).astype(np.float64)
    return np.moveaxis((codes * scale).reshape(v.shape), -1, axis)


WIDE = False


def mx_kscale(k):
    if not WIDE:
        return np.ones(k)
    levels = np.array([10, -10, 5, -5, 0])
    if k % 512:
        return np.exp2(np.random.permutation(np.resize(levels, k // 32))).repeat(32)
    a = np.empty((k // 512, 16))
    for p in range(k // 512):
        a[p, :8] = np.random.permutation(np.resize(levels, 8))
        for g in range(8):
            far = levels[np.abs(levels - a[p, g]) >= 10]
            a[p, g + 8] = far[np.random.randint(len(far))]
    return np.exp2(a.ravel()).repeat(32)


BF16 = ml_dtypes.bfloat16


def bf(x):
    return np.asarray(x, np.float32).astype(BF16)


def f64(x):
    return np.asarray(x).astype(np.float64)


E2M1 = np.array([0.0, 0.5, 1.0, 1.5, 2.0, 3.0, 4.0, 6.0, -0.0, -0.5, -1.0, -1.5, -2.0, -3.0, -4.0, -6.0])


def pack_weight(w, fmt):
    k, n = w.shape
    w = f64(bf(w)).reshape(k // 32, 32, n)
    amax = np.abs(w).max(1)
    if fmt == "e4m3":
        byte = np.frexp(amax)[1] - 1 + 127 - 7
    else:
        mant, ex = np.frexp(amax / 6.0)
        byte = np.where(mant > 0.5, ex, ex - 1) + 127
    byte = np.clip(np.where(amax > 0, byte, 1), 1, 254)
    scaled = (w * np.exp2(127.0 - byte)[:, None, :]).reshape(k, n).astype(np.float32)
    by_word = np.ascontiguousarray(scaled.reshape(k // 512, 128, 4, n).transpose(0, 1, 3, 2))
    if fmt == "e4m3":
        words = by_word.astype(ml_dtypes.float8_e4m3fn).view(np.uint8)
    else:
        c = by_word.astype(ml_dtypes.float4_e2m1fn).view(np.uint8) & 0xF
        words = c[..., 0::2] | (c[..., 1::2] << 4)
    return np.ascontiguousarray(words), np.ascontiguousarray(byte.astype(np.uint8).reshape(k // 512, 16, n))


def unpack_weight(words, scales, fmt):
    g, p, n, _ = words.shape
    if fmt == "e4m3":
        vals = np.ascontiguousarray(words).view(ml_dtypes.float8_e4m3fn).astype(np.float64)
    else:
        nib = np.empty((g, p, n, 4), np.uint8)
        nib[..., 0::2] = words & 0xF
        nib[..., 1::2] = words >> 4
        vals = E2M1[nib]
    vals = vals * np.repeat(np.exp2(scales.astype(np.float64) - 127.0), 8, axis=1)[..., None]
    return vals.transpose(0, 1, 3, 2).reshape(g * 512, n)
def pack4(w):
    words, scales = pack_weight(w, "e2m1")
    return words.reshape(words.shape[0], 128, -1), scales


def unpack4(words, scales):
    return unpack_weight(words.reshape(words.shape[0], 128, -1, 2), scales, "e2m1")


E4M3FN = np.array([(-1.0 if i & 128 else 1.0) * ((1.0 + (i & 7) / 8.0) * 2.0 ** (((i >> 3) & 15) - 7) if i & 120 else (i & 7) * 2.0 ** -9) for i in range(256)])


def e4m3fn_bytes(y):
    return np.clip(np.asarray(y, np.float64), -448.0, 448.0).astype(np.float32).astype(ml_dtypes.float8_e4m3fn).view(np.uint8)


def e4m3fn_values(b):
    return E4M3FN[b]


T, K, NQ, NI, D, B = 1024, 1536, 2048, 1024, 128, 128


def setup_inputs():
    s = mx_kscale(K)
    c = np.random.standard_normal((T, K)) * s
    w = np.random.standard_normal((NQ, K)) / np.sqrt(K) / s
    v = np.random.standard_normal((K, NI)) / np.sqrt(K) / s[:, None]
    c_scale = (np.abs(c).reshape(T, K // B, B).max(axis=2) / 448).astype(np.float32)
    w_scale = (np.abs(w).reshape(NQ // B, B, K // B, B).max(axis=(1, 3)) / 448).astype(np.float32)
    c_bytes = e4m3fn_bytes(c / np.repeat(f64(c_scale), B, axis=1))
    w_bytes = e4m3fn_bytes(w / np.repeat(np.repeat(f64(w_scale), B, axis=0), B, axis=1))
    v_words, v_scales = pack4(v)
    return {"c_bytes": c_bytes, "c_scale": c_scale,
            "w_bytes": w_bytes, "w_scale": w_scale,
            "v_words": v_words, "v_scales": v_scales,
            "bias": bf(0.3 * np.random.standard_normal(NQ)),
            "head_gain": bf(1 + 0.3 * np.random.standard_normal((T, NI // D)))}


def reference(c_bytes, c_scale, w_bytes, w_scale, v_words, v_scales, bias, head_gain):
    c = e4m3fn_values(c_bytes) * np.repeat(f64(c_scale), B, axis=1)
    w = e4m3fn_values(w_bytes) * np.repeat(np.repeat(f64(w_scale), B, axis=0), B, axis=1)
    cq = mxq(c, 1, "e4m3")
    wq = mxq(w, 1, "e4m3")
    main = (cq @ wq.T) + f64(bias)
    index = cq @ unpack4(v_words, v_scales)
    index = index.reshape(T, NI // D, D) * f64(head_gain)[:, :, None]
    return main, index.reshape(T, NI)

@@ -1,0 +1,277 @@
+from contextlib import ExitStack
+
+import concourse.mybir as mybir
+from concourse.masks import make_identity
+
+T, K, NQ, NI, D, B = 1024, 1536, 2048, 1024, 128, 128
+FLOPS = 2 * T * K * (NQ + NI)
+
+F32 = mybir.dt.float32
+BF16 = mybir.dt.bfloat16
+I32 = mybir.dt.int32
+U32 = mybir.dt.uint32
+U8 = mybir.dt.uint8
+FP8 = mybir.dt.float8_e4m3fn
+FP8X4 = mybir.dt.float8_e4m3fn_x4
+FP4X4 = mybir.dt.float4_e2m1fn_x4
+MULT = mybir.AluOpType.mult
+ADD = mybir.AluOpType.add
+COPY = mybir.ActivationFunctionType.Copy
+
+P = 128
+K_PASS = 512
+PASSES = K // K_PASS
+BLOCKS = K // B
+BLOCKS_PER_PASS = K_PASS // B
+TOKEN_TILES = T // P
+HEADS = NI // D
+PAIR = 2
+PAIR_ROWS = PAIR * P
+C_PAIRS = T // PAIR_ROWS
+W_PAIRS = NQ // PAIR_ROWS
+PAIRS = C_PAIRS + W_PAIRS
+BANK = 512
+BANKS_PER_STEP = 4
+ACC_BANKS = 5
+WIDE_RING = 30
+GROUPED_RING = 6
+STAGE_RING = 16
+WIDEN_C_STEP = 10
+WIDEN_W_STEP = 4
+
+
+def tile_latent_query_up_projection_d6_kernel(
+    tc, c_bytes, c_scale, w_bytes, w_scale, v_words, v_scales, bias, head_gain, out_0, out_1
+):
+    nc = tc.nc
+    with ExitStack() as ctx:
+        keep = ctx.enter_context(tc.tile_pool(name="keep", bufs=1))
+        psum = ctx.enter_context(tc.psum_pool(name="psum", bufs=1))
+        ctx.enter_context(tc.manual_schedule())
+
+        ident = keep.tile([P, P], F32, name="ident")
+        make_identity(nc, ident[:])
+
+        v_plane = keep.tile([P, PASSES * NI], U8, name="v_plane", align_bytes=64)
+        nc.vector.memset(v_plane[:].bitcast(I32), 0)
+
+        c_rows = c_bytes.rearrange("(p i) k -> p i k", i=TOKEN_TILES)
+        raw = {}
+
+        c_scale_sb = keep.tile([P, TOKEN_TILES * BLOCKS], F32, name="c_scale_sb")
+        nc.sync.dma_start(out=c_scale_sb[:], in_=c_scale.rearrange("(p i) j -> p (i j)", i=TOKEN_TILES))
+
+        for g in range(PASSES):
+            piece = keep.tile([P, PAIR, K_PASS], U8, name="c_raw_first%d" % g)
+            nc.sync.dma_start(out=piece[:], in_=c_rows[:, 0:PAIR, g * K_PASS : (g + 1) * K_PASS])
+            for a in range(PAIR):
+                raw[(0, a, g)] = piece[:, a, :]
+
+        def load_pair(r):
+            if r < C_PAIRS:
+                rows = keep.tile([P, PAIR, K], U8, name="c_raw%d" % r)
+                src = c_rows[:, PAIR * r : PAIR * (r + 1), :]
+            else:
+                rows = keep.tile([P, PAIR, K], U8, name="w_raw%d" % r)
+                n0 = (r - C_PAIRS) * PAIR_ROWS
+                src = w_bytes[n0 : n0 + PAIR_ROWS, :].rearrange("(a p) k -> p a k", p=P)
+            nc.sync.dma_start(out=rows[:], in_=src)
+            for a in range(PAIR):
+                for g in range(PASSES):
+                    raw[(r, a, g)] = rows[:, a, g * K_PASS : (g + 1) * K_PASS]
+
+        v_codes = []
+
+        def load_v_half(h):
+            words = keep.tile([P, PASSES, 2 * BANK], U8, name="v_codes%d" % h, align_bytes=64)
+            src = v_words.rearrange("g p n -> p g n")[:, :, 2 * BANK * h : 2 * BANK * (h + 1)]
+            nc.sync.dma_start(out=words[:].bitcast(I32), in_=src.bitcast(I32))
+            v_codes.append(words)
+
+        load_v_half(0)
+        v_plane_3d = v_plane[:].rearrange("p (g n) -> p g n", g=PASSES)
+        for quad in range(4):
+            nc.sync.dma_start(
+                out=v_plane_3d[32 * quad : 32 * quad + 4, :, :].bitcast(I32),
+                in_=v_scales.rearrange("g q n -> q g n")[4 * quad : 4 * quad + 4, :, :].bitcast(I32),
+            )
+        load_v_half(1)
+        load_pair(1)
+        gain_bf = keep.tile([P, TOKEN_TILES * HEADS], BF16, name="gain_bf")
+        nc.sync.dma_start(out=gain_bf[:], in_=head_gain.rearrange("(p i) h -> p (i h)", i=TOKEN_TILES))
+        gain = keep.tile([P, TOKEN_TILES * HEADS], F32, name="gain")
+        nc.gpsimd.tensor_copy(out=gain[:], in_=gain_bf[:])
+        for r in range(2, C_PAIRS):
+            load_pair(r)
+        w_scale_sb = keep.tile([P, (NQ // B) * BLOCKS], F32, name="w_scale_sb")
+        nc.sync.dma_start(out=w_scale_sb[:], in_=w_scale.rearrange("a j -> (a j)").partition_broadcast(P))
+        for r in range(C_PAIRS, PAIRS):
+            load_pair(r)
+        bias_sb = keep.tile([P, NQ], BF16, name="bias_sb")
+        nc.sync.dma_start(out=bias_sb[:], in_=bias.partition_broadcast(P))
+
+        order = [(r, a, g) for r in range(PAIRS) for g in range(PASSES) for a in range(PAIR)]
+        wide = {}
+        grouped = {}
+        codes = {}
+        planes = {}
+
+        def widen(count):
+            for n in range(len(wide), min(len(wide) + count, len(order))):
+                r, a, g = order[n]
+                dst = keep.tile([P, K_PASS], BF16, name="wide%d" % (n % WIDE_RING), align_bytes=64)
+                split = dst[:].rearrange("p (u m e) -> p m u e", u=2, e=2)
+                for q in range(BLOCKS_PER_PASS):
+                    j = g * BLOCKS_PER_PASS + q
+                    if r < C_PAIRS:
+                        col = (PAIR * r + a) * BLOCKS + j
+                        scale = c_scale_sb[:, col : col + 1]
+                    else:
+                        col = (PAIR * (r - C_PAIRS) + a) * BLOCKS + j
+                        scale = w_scale_sb[:, col : col + 1]
+                    src = raw[(r, a, g)][:, q * B : (q + 1) * B].bitcast(FP8)
+                    nc.vector.tensor_scalar(
+                        out=split[:, 32 * q : 32 * (q + 1), :, :],
+                        in0=src.rearrange("p (m u e) -> p m u e", u=2, e=2),
+                        scalar1=scale,
+                        scalar2=None,
+                        op0=MULT,
+                    )
+                wide[(r, a, g)] = dst
+
+        def turn(r, g):
+            bank = psum.tile([P, PAIR, 2, P], F32, name="turn%d" % g)
+            for a in range(PAIR):
+                words = wide[(r, a, g)][:].bitcast(F32)
+                for u in range(2):
+                    nc.tensor.transpose(bank[:, a, u, :], words[:, u * P : (u + 1) * P], ident[:])
+            dst = keep.tile(
+                [P, PAIR_ROWS * 4], BF16, name="grouped%d" % ((r * PASSES + g) % GROUPED_RING), align_bytes=64
+            )
+            nc.scalar.copy(
+                out=dst[:].bitcast(F32).rearrange("p (a r u) -> p a r u", a=PAIR, u=2),
+                in_=bank[:].rearrange("p a u r -> p a r u"),
+            )
+            grouped[(r, g)] = dst
+
+        def quantize(r, g):
+            words = keep.tile([P, PAIR_ROWS], U32, name="codes%d_%d" % (r, g), align_bytes=64)
+            plane = keep.tile([P, PAIR_ROWS], U8, name="plane%d_%d" % (r, g), align_bytes=64)
+            nc.vector.quantize_mx(out=words[:].bitcast(FP8X4), scales=plane[:], in_=grouped[(r, g)][:])
+            codes[(r, g)] = words
+            planes[(r, g)] = plane
+
+        acc = {}
+        main_rows = out_0.rearrange("(p i) n -> p i n", i=TOKEN_TILES)
+        index_rows = out_1.rearrange("(p i) n -> p i n", i=TOKEN_TILES)
+
+        def multiply(s, b):
+            bank = psum.tile([P, BANK], F32, name="acc%d" % ((s * BANKS_PER_STEP + b) % ACC_BANKS))
+            if s < C_PAIRS:
+                a, h = divmod(b, 2)
+                for g in range(PASSES):
+                    nc.tensor.matmul_mx(
+                        out=bank[:],
+                        lhsT=codes[(s, g)][:, a * P : (a + 1) * P].bitcast(FP8X4),
+                        lhsT_scale=planes[(s, g)][:, a * P : (a + 1) * P],
+                        rhs=v_codes[h][:, g, :].bitcast(FP4X4),
+                        rhs_scale=v_plane[:, g * NI + h * BANK : g * NI + (h + 1) * BANK],
+                        start=(g == 0),
+                        stop=(g == PASSES - 1),
+                    )
+            else:
+                for a in range(PAIR):
+                    for g in range(PASSES):
+                        nc.tensor.matmul_mx(
+                            out=bank[:, a * PAIR_ROWS : (a + 1) * PAIR_ROWS],
+                            lhsT=codes[(b, g)][:, a * P : (a + 1) * P].bitcast(FP8X4),
+                            lhsT_scale=planes[(b, g)][:, a * P : (a + 1) * P],
+                            rhs=codes[(s, g)][:].bitcast(FP8X4),
+                            rhs_scale=planes[(s, g)][:],
+                            start=(g == 0),
+                            stop=(g == PASSES - 1),
+                        )
+            acc[(s, b)] = bank
+
+        def finish(s, b):
+            bank = acc[(s, b)]
+            stage = keep.tile([P, BANK], F32, name="stage%d" % ((s * BANKS_PER_STEP + b) % STAGE_RING))
+            if s < C_PAIRS:
+                a, h = divmod(b, 2)
+                i = PAIR * s + a
+                heads = BANK // D
+                first = i * HEADS + h * heads
+                if b == BANKS_PER_STEP - 1:
+                    nc.vector.tensor_tensor(
+                        out=stage[:].rearrange("p (h d) -> p h d", d=D),
+                        in0=bank[:].rearrange("p (h d) -> p h d", d=D),
+                        in1=gain[:, first : first + heads].unsqueeze(2).to_broadcast([P, heads, D]),
+                        op=MULT,
+                    )
+                else:
+                    for e in range(heads):
+                        nc.scalar.activation(
+                            out=stage[:, e * D : (e + 1) * D],
+                            in_=bank[:, e * D : (e + 1) * D],
+                            func=COPY,
+                            scale=gain[:, first + e : first + e + 1],
+                        )
+                nc.sync.dma_start(out=index_rows[:, i, h * BANK : (h + 1) * BANK], in_=stage[:])
+            else:
+                n0 = (s - C_PAIRS) * PAIR_ROWS
+                both = stage[:].rearrange("p (a n) -> p a n", a=PAIR)
+                nc.vector.tensor_tensor(
+                    out=both,
+                    in0=bank[:].rearrange("p (a n) -> p a n", a=PAIR),
+                    in1=bias_sb[:, n0 : n0 + PAIR_ROWS].unsqueeze(1).to_broadcast([P, PAIR, PAIR_ROWS]),
+                    op=ADD,
+                )
+                nc.sync.dma_start(out=main_rows[:, PAIR * b : PAIR * (b + 1), n0 : n0 + PAIR_ROWS], in_=both)
+
+        for g in range(PASSES):
+            widen(PAIR)
+            turn(0, g)
+        quantize(0, 0)
+        quantize(0, 1)
+        widen(1)
+        quantize(0, 2)
+        widen(PAIR * PASSES - 1)
+        for b in range(2):
+            multiply(0, b)
+            finish(0, b)
+        for g in range(PASSES):
+            turn(1, g)
+        for g in range(PASSES):
+            widen(PAIR)
+            quantize(1, g)
+        multiply(0, 2)
+        finish(0, 2)
+        multiply(0, 3)
+
+        for s in range(1, PAIRS):
+            ahead = s + 1 < PAIRS
+            extra = WIDEN_C_STEP - WIDEN_W_STEP if s < C_PAIRS else 0
+            if ahead:
+                for g in range(PASSES):
+                    turn(s + 1, g)
+            finish(s - 1, BANKS_PER_STEP - 1)
+            widen(1)
+            if ahead:
+                quantize(s + 1, 0)
+            widen(1)
+            if ahead:
+                quantize(s + 1, 1)
+            multiply(s, 0)
+            finish(s, 0)
+            if s < C_PAIRS:
+                widen(1)
+            if ahead:
+                quantize(s + 1, 2)
+            widen(1)
+            multiply(s, 1)
+            finish(s, 1)
+            widen(1 + max(extra - 1, 0))
+            multiply(s, 2)
+            finish(s, 2)
+            multiply(s, 3)
+        finish(PAIRS - 1, BANKS_PER_STEP - 1)

@@ -33,11 +33,9 @@ PAIRS = C_PAIRS + W_PAIRS
 BANK = 512
 BANKS_PER_STEP = 4
 ACC_BANKS = 5
-WIDE_RING = 30
+WIDE_RING = 18
 GROUPED_RING = 6
 STAGE_RING = 16
-WIDEN_C_STEP = 10
-WIDEN_W_STEP = 4
 
 
 def tile_latent_query_up_projection_d6_kernel(
@@ -55,17 +53,17 @@ def tile_latent_query_up_projection_d6_kernel(
         v_plane = keep.tile([P, PASSES * NI], U8, name="v_plane", align_bytes=64)
         nc.vector.memset(v_plane[:].bitcast(I32), 0)
 
+        warm_bank = psum.tile([P, BANK], F32, name="acc%d" % (ACC_BANKS - 1))
+
+        def warm_up(count):
+            for n in range(count):
+                nc.tensor.matmul(warm_bank[:, 0:P], lhsT=ident[:], rhs=ident[:], start=True, stop=True)
+
         c_rows = c_bytes.rearrange("(p i) k -> p i k", i=TOKEN_TILES)
         raw = {}
 
         c_scale_sb = keep.tile([P, TOKEN_TILES * BLOCKS], F32, name="c_scale_sb")
         nc.sync.dma_start(out=c_scale_sb[:], in_=c_scale.rearrange("(p i) j -> p (i j)", i=TOKEN_TILES))
-
-        for g in range(PASSES):
-            piece = keep.tile([P, PAIR, K_PASS], U8, name="c_raw_first%d" % g)
-            nc.sync.dma_start(out=piece[:], in_=c_rows[:, 0:PAIR, g * K_PASS : (g + 1) * K_PASS])
-            for a in range(PAIR):
-                raw[(0, a, g)] = piece[:, a, :]
 
         def load_pair(r):
             if r < C_PAIRS:
@@ -88,6 +86,13 @@ def tile_latent_query_up_projection_d6_kernel(
             nc.sync.dma_start(out=words[:].bitcast(I32), in_=src.bitcast(I32))
             v_codes.append(words)
 
+        for g0, g1 in ((0, 1), (1, PASSES)):
+            piece = keep.tile([P, PAIR, (g1 - g0) * K_PASS], U8, name="c_raw_first%d" % g0)
+            nc.sync.dma_start(out=piece[:], in_=c_rows[:, 0:PAIR, g0 * K_PASS : g1 * K_PASS])
+            for a in range(PAIR):
+                for g in range(g0, g1):
+                    raw[(0, a, g)] = piece[:, a, (g - g0) * K_PASS : (g - g0 + 1) * K_PASS]
+        load_pair(1)
         load_v_half(0)
         v_plane_3d = v_plane[:].rearrange("p (g n) -> p g n", g=PASSES)
         for quad in range(4):
@@ -96,12 +101,12 @@ def tile_latent_query_up_projection_d6_kernel(
                 in_=v_scales.rearrange("g q n -> q g n")[4 * quad : 4 * quad + 4, :, :].bitcast(I32),
             )
         load_v_half(1)
-        load_pair(1)
+        load_pair(2)
         gain_bf = keep.tile([P, TOKEN_TILES * HEADS], BF16, name="gain_bf")
         nc.sync.dma_start(out=gain_bf[:], in_=head_gain.rearrange("(p i) h -> p (i h)", i=TOKEN_TILES))
         gain = keep.tile([P, TOKEN_TILES * HEADS], F32, name="gain")
         nc.gpsimd.tensor_copy(out=gain[:], in_=gain_bf[:])
-        for r in range(2, C_PAIRS):
+        for r in range(3, C_PAIRS):
             load_pair(r)
         w_scale_sb = keep.tile([P, (NQ // B) * BLOCKS], F32, name="w_scale_sb")
         nc.sync.dma_start(out=w_scale_sb[:], in_=w_scale.rearrange("a j -> (a j)").partition_broadcast(P))
@@ -110,26 +115,31 @@ def tile_latent_query_up_projection_d6_kernel(
         bias_sb = keep.tile([P, NQ], BF16, name="bias_sb")
         nc.sync.dma_start(out=bias_sb[:], in_=bias.partition_broadcast(P))
 
-        order = [(r, a, g) for r in range(PAIRS) for g in range(PASSES) for a in range(PAIR)]
         wide = {}
         grouped = {}
         codes = {}
         planes = {}
 
-        def widen(count):
-            for n in range(len(wide), min(len(wide) + count, len(order))):
-                r, a, g = order[n]
-                dst = keep.tile([P, K_PASS], BF16, name="wide%d" % (n % WIDE_RING), align_bytes=64)
-                split = dst[:].rearrange("p (u m e) -> p m u e", u=2, e=2)
-                for q in range(BLOCKS_PER_PASS):
-                    j = g * BLOCKS_PER_PASS + q
-                    if r < C_PAIRS:
-                        col = (PAIR * r + a) * BLOCKS + j
-                        scale = c_scale_sb[:, col : col + 1]
-                    else:
-                        col = (PAIR * (r - C_PAIRS) + a) * BLOCKS + j
-                        scale = w_scale_sb[:, col : col + 1]
-                    src = raw[(r, a, g)][:, q * B : (q + 1) * B].bitcast(FP8)
+        def on_scalar(r, a, g):
+            return a == 1 and (g < 2 if r < 2 else r >= C_PAIRS + 2)
+
+        def widen(r, a, g):
+            dst = keep.tile(
+                [P, K_PASS], BF16, name="wide%d" % (((r * PASSES + g) * PAIR + a) % WIDE_RING), align_bytes=64
+            )
+            split = dst[:].rearrange("p (u m e) -> p m u e", u=2, e=2)
+            for q in range(BLOCKS_PER_PASS):
+                j = g * BLOCKS_PER_PASS + q
+                if r < C_PAIRS:
+                    col = (PAIR * r + a) * BLOCKS + j
+                    scale = c_scale_sb[:, col : col + 1]
+                else:
+                    col = (PAIR * (r - C_PAIRS) + a) * BLOCKS + j
+                    scale = w_scale_sb[:, col : col + 1]
+                src = raw[(r, a, g)][:, q * B : (q + 1) * B].bitcast(FP8)
+                if on_scalar(r, a, g):
+                    nc.scalar.activation(out=dst[:, q * B : (q + 1) * B], in_=src, func=COPY, scale=scale)
+                else:
                     nc.vector.tensor_scalar(
                         out=split[:, 32 * q : 32 * (q + 1), :, :],
                         in0=src.rearrange("p (m u e) -> p m u e", u=2, e=2),
@@ -137,14 +147,20 @@ def tile_latent_query_up_projection_d6_kernel(
                         scalar2=None,
                         op0=MULT,
                     )
-                wide[(r, a, g)] = dst
+            wide[(r, a, g)] = dst
+
+        def widen_pass(r, g):
+            if r < PAIRS:
+                for a in range(PAIR):
+                    widen(r, a, g)
 
         def turn(r, g):
             bank = psum.tile([P, PAIR, 2, P], F32, name="turn%d" % g)
             for a in range(PAIR):
                 words = wide[(r, a, g)][:].bitcast(F32)
                 for u in range(2):
-                    nc.tensor.transpose(bank[:, a, u, :], words[:, u * P : (u + 1) * P], ident[:])
+                    half = words[:, u : 2 * P : 2] if on_scalar(r, a, g) else words[:, u * P : (u + 1) * P]
+                    nc.tensor.transpose(bank[:, a, u, :], half, ident[:])
             dst = keep.tile(
                 [P, PAIR_ROWS * 4], BF16, name="grouped%d" % ((r * PASSES + g) % GROUPED_RING), align_bytes=64
             )
@@ -165,8 +181,8 @@ def tile_latent_query_up_projection_d6_kernel(
         main_rows = out_0.rearrange("(p i) n -> p i n", i=TOKEN_TILES)
         index_rows = out_1.rearrange("(p i) n -> p i n", i=TOKEN_TILES)
 
-        def multiply(s, b):
-            bank = psum.tile([P, BANK], F32, name="acc%d" % ((s * BANKS_PER_STEP + b) % ACC_BANKS))
+        def multiply(s, b, tiles=(0, 1)):
+            bank = psum.tile([P, BANK], F32, name="acc%d" % (len(acc) % ACC_BANKS))
             if s < C_PAIRS:
                 a, h = divmod(b, 2)
                 for g in range(PASSES):
@@ -180,7 +196,7 @@ def tile_latent_query_up_projection_d6_kernel(
                         stop=(g == PASSES - 1),
                     )
             else:
-                for a in range(PAIR):
+                for a in tiles:
                     for g in range(PASSES):
                         nc.tensor.matmul_mx(
                             out=bank[:, a * PAIR_ROWS : (a + 1) * PAIR_ROWS],
@@ -191,11 +207,11 @@ def tile_latent_query_up_projection_d6_kernel(
                             start=(g == 0),
                             stop=(g == PASSES - 1),
                         )
-            acc[(s, b)] = bank
+            acc[(s, b, tiles)] = (bank, len(acc))
 
-        def finish(s, b):
-            bank = acc[(s, b)]
-            stage = keep.tile([P, BANK], F32, name="stage%d" % ((s * BANKS_PER_STEP + b) % STAGE_RING))
+        def finish(s, b, tiles=(0, 1)):
+            bank, number = acc[(s, b, tiles)]
+            stage = keep.tile([P, BANK], F32, name="stage%d" % (number % STAGE_RING))
             if s < C_PAIRS:
                 a, h = divmod(b, 2)
                 i = PAIR * s + a
@@ -219,59 +235,78 @@ def tile_latent_query_up_projection_d6_kernel(
                 nc.sync.dma_start(out=index_rows[:, i, h * BANK : (h + 1) * BANK], in_=stage[:])
             else:
                 n0 = (s - C_PAIRS) * PAIR_ROWS
-                both = stage[:].rearrange("p (a n) -> p a n", a=PAIR)
+                a0, a1 = tiles[0], tiles[-1] + 1
+                rows = stage[:].rearrange("p (a n) -> p a n", a=PAIR)[:, a0:a1, :]
                 nc.vector.tensor_tensor(
-                    out=both,
-                    in0=bank[:].rearrange("p (a n) -> p a n", a=PAIR),
-                    in1=bias_sb[:, n0 : n0 + PAIR_ROWS].unsqueeze(1).to_broadcast([P, PAIR, PAIR_ROWS]),
+                    out=rows,
+                    in0=bank[:].rearrange("p (a n) -> p a n", a=PAIR)[:, a0:a1, :],
+                    in1=bias_sb[:, n0 : n0 + PAIR_ROWS].unsqueeze(1).to_broadcast([P, a1 - a0, PAIR_ROWS]),
                     op=ADD,
                 )
-                nc.sync.dma_start(out=main_rows[:, PAIR * b : PAIR * (b + 1), n0 : n0 + PAIR_ROWS], in_=both)
+                nc.sync.dma_start(out=main_rows[:, PAIR * b + a0 : PAIR * b + a1, n0 : n0 + PAIR_ROWS], in_=rows)
 
+        warm_up(4)
         for g in range(PASSES):
-            widen(PAIR)
+            widen_pass(0, g)
+        for g in range(PASSES):
             turn(0, g)
+        warm_up(2)
         quantize(0, 0)
+        widen(1, 0, 0)
         quantize(0, 1)
-        widen(1)
         quantize(0, 2)
-        widen(PAIR * PASSES - 1)
-        for b in range(2):
-            multiply(0, b)
-            finish(0, b)
+        widen(1, 0, 1)
+        widen(1, 0, 2)
+        for g in range(PASSES):
+            widen(1, 1, g)
+        multiply(0, 0)
         for g in range(PASSES):
             turn(1, g)
-        for g in range(PASSES):
-            widen(PAIR)
-            quantize(1, g)
+        multiply(0, 1)
+        widen_pass(2, 0)
+        widen_pass(2, 1)
+        quantize(1, 0)
+        widen(2, 0, 2)
+        quantize(1, 1)
+        widen(2, 1, 2)
+        quantize(1, 2)
         multiply(0, 2)
-        finish(0, 2)
         multiply(0, 3)
+        for b in range(3):
+            finish(0, b)
 
         for s in range(1, PAIRS):
             ahead = s + 1 < PAIRS
-            extra = WIDEN_C_STEP - WIDEN_W_STEP if s < C_PAIRS else 0
+            later = s + 2 < PAIRS
             if ahead:
                 for g in range(PASSES):
                     turn(s + 1, g)
             finish(s - 1, BANKS_PER_STEP - 1)
-            widen(1)
+            if later:
+                widen(s + 2, 0, 0)
             if ahead:
                 quantize(s + 1, 0)
-            widen(1)
+            if later:
+                widen(s + 2, 0, 1)
             if ahead:
                 quantize(s + 1, 1)
+            if later:
+                widen(s + 2, 1, 0)
             multiply(s, 0)
             finish(s, 0)
-            if s < C_PAIRS:
-                widen(1)
             if ahead:
                 quantize(s + 1, 2)
-            widen(1)
+            if later:
+                widen(s + 2, 0, 2)
+                widen(s + 2, 1, 1)
             multiply(s, 1)
             finish(s, 1)
-            widen(1 + max(extra - 1, 0))
+            if later:
+                widen(s + 2, 1, 2)
             multiply(s, 2)
             finish(s, 2)
-            multiply(s, 3)
-        finish(PAIRS - 1, BANKS_PER_STEP - 1)
+            if ahead:
+                multiply(s, 3)
+        for a in range(PAIR):
+            multiply(PAIRS - 1, BANKS_PER_STEP - 1, (a,))
+            finish(PAIRS - 1, BANKS_PER_STEP - 1, (a,))

@@ -35,7 +35,7 @@ BANKS_PER_STEP = 4
 ACC_BANKS = 5
 WIDE_RING = 18
 GROUPED_RING = 6
-STAGE_RING = 16
+STAGE_RING = 24
 
 
 def tile_latent_query_up_projection_d6_kernel(
@@ -116,18 +116,22 @@ def tile_latent_query_up_projection_d6_kernel(
         nc.sync.dma_start(out=bias_sb[:], in_=bias.partition_broadcast(P))
 
         wide = {}
+        flat = {}
         grouped = {}
         codes = {}
         planes = {}
 
         def on_scalar(r, a, g):
-            return a == 1 and (g < 2 if r < 2 else r >= C_PAIRS + 2)
+            return a == 1 and (g < 2 if r < 2 else r >= C_PAIRS + 2 and g < 2 + r % 2)
 
         def widen(r, a, g):
             dst = keep.tile(
                 [P, K_PASS], BF16, name="wide%d" % (((r * PASSES + g) * PAIR + a) % WIDE_RING), align_bytes=64
             )
             split = dst[:].rearrange("p (u m e) -> p m u e", u=2, e=2)
+            if on_scalar(r, a, g) and r >= C_PAIRS:
+                flat[(r, g)] = keep.tile([P, K_PASS], BF16, name="flat%d" % g, align_bytes=64)
+            plain = flat.get((r, g), dst)
             for q in range(BLOCKS_PER_PASS):
                 j = g * BLOCKS_PER_PASS + q
                 if r < C_PAIRS:
@@ -138,7 +142,7 @@ def tile_latent_query_up_projection_d6_kernel(
                     scale = w_scale_sb[:, col : col + 1]
                 src = raw[(r, a, g)][:, q * B : (q + 1) * B].bitcast(FP8)
                 if on_scalar(r, a, g):
-                    nc.scalar.activation(out=dst[:, q * B : (q + 1) * B], in_=src, func=COPY, scale=scale)
+                    nc.scalar.activation(out=plain[:, q * B : (q + 1) * B], in_=src, func=COPY, scale=scale)
                 else:
                     nc.vector.tensor_scalar(
                         out=split[:, 32 * q : 32 * (q + 1), :, :],
@@ -148,6 +152,13 @@ def tile_latent_query_up_projection_d6_kernel(
                         op0=MULT,
                     )
             wide[(r, a, g)] = dst
+
+        def part_words(r, g):
+            if (r, g) in flat:
+                nc.scalar.copy(
+                    out=wide[(r, 1, g)][:].bitcast(F32).rearrange("p (u m) -> p u m", u=2),
+                    in_=flat[(r, g)][:].bitcast(F32).rearrange("p (m u) -> p u m", u=2),
+                )
 
         def widen_pass(r, g):
             if r < PAIRS:
@@ -159,7 +170,7 @@ def tile_latent_query_up_projection_d6_kernel(
             for a in range(PAIR):
                 words = wide[(r, a, g)][:].bitcast(F32)
                 for u in range(2):
-                    half = words[:, u : 2 * P : 2] if on_scalar(r, a, g) else words[:, u * P : (u + 1) * P]
+                    half = words[:, u : 2 * P : 2] if on_scalar(r, a, g) and r < C_PAIRS else words[:, u * P : (u + 1) * P]
                     nc.tensor.transpose(bank[:, a, u, :], half, ident[:])
             dst = keep.tile(
                 [P, PAIR_ROWS * 4], BF16, name="grouped%d" % ((r * PASSES + g) % GROUPED_RING), align_bytes=64
@@ -299,10 +310,13 @@ def tile_latent_query_up_projection_d6_kernel(
             if later:
                 widen(s + 2, 0, 2)
                 widen(s + 2, 1, 1)
+                part_words(s + 2, 0)
             multiply(s, 1)
             finish(s, 1)
             if later:
                 widen(s + 2, 1, 2)
+                part_words(s + 2, 1)
+                part_words(s + 2, 2)
             multiply(s, 2)
             finish(s, 2)
             if ahead:

@@ -19,23 +19,50 @@ ADD = mybir.AluOpType.add
 COPY = mybir.ActivationFunctionType.Copy
 
 P = 128
-K_PASS = 512
+PACK = 4
+K_PASS = P * PACK
 PASSES = K // K_PASS
-BLOCKS = K // B
-BLOCKS_PER_PASS = K_PASS // B
+SCALE_COLS = K // B
+SCALES_PER_PASS = K_PASS // B
 TOKEN_TILES = T // P
 HEADS = NI // D
+BANK = 512
+HEADS_PER_BANK = BANK // D
 PAIR = 2
 PAIR_ROWS = PAIR * P
 C_PAIRS = T // PAIR_ROWS
-W_PAIRS = NQ // PAIR_ROWS
-PAIRS = C_PAIRS + W_PAIRS
-BANK = 512
-BANKS_PER_STEP = 4
-ACC_BANKS = 5
-WIDE_RING = 18
-GROUPED_RING = 6
-STAGE_RING = 24
+PAIRS = C_PAIRS + NQ // PAIR_ROWS
+CHUNKS = NQ // BANK
+PAIRS_PER_CHUNK = BANK // PAIR_ROWS
+INDEX_BANKS = PAIR * NI // BANK
+
+PSUM_BANKS = 8
+WIDE_RING = 24
+FLAT_RING = 4
+TURNED_RING = 4
+STAGE_RING = 20
+
+WARM_FIRST, WARM_SECOND = 4, 2
+WIDEN_PER_C_STEP = 9
+TURN_AT = TOKEN_TILES // 2
+
+
+def scalar_passes(r):
+    if r < 2:
+        return 2
+    if r < C_PAIRS + PAIRS_PER_CHUNK:
+        return 0
+    if r < C_PAIRS + 2 * PAIRS_PER_CHUNK:
+        return 1
+    return 2 + r % 2
+
+
+def on_scalar(r, a, g):
+    return a == 1 and g < scalar_passes(r)
+
+
+def chunk_pairs(j):
+    return range(C_PAIRS + PAIRS_PER_CHUNK * j, C_PAIRS + PAIRS_PER_CHUNK * (j + 1))
 
 
 def tile_latent_query_up_projection_d6_kernel(
@@ -43,200 +70,189 @@ def tile_latent_query_up_projection_d6_kernel(
 ):
     nc = tc.nc
     with ExitStack() as ctx:
-        keep = ctx.enter_context(tc.tile_pool(name="keep", bufs=1))
+        sbuf = ctx.enter_context(tc.tile_pool(name="sbuf", bufs=1))
         psum = ctx.enter_context(tc.psum_pool(name="psum", bufs=1))
         ctx.enter_context(tc.manual_schedule())
 
-        ident = keep.tile([P, P], F32, name="ident")
+        ident = sbuf.tile([P, P], F32, name="ident")
         make_identity(nc, ident[:])
 
-        v_plane = keep.tile([P, PASSES * NI], U8, name="v_plane", align_bytes=64)
+        v_plane = sbuf.tile([P, PASSES * NI], U8, name="v_plane", align_bytes=64)
         nc.vector.memset(v_plane[:].bitcast(I32), 0)
 
-        warm_bank = psum.tile([P, BANK], F32, name="acc%d" % (ACC_BANKS - 1))
+        banks_taken = []
 
-        def warm_up(count):
-            for n in range(count):
-                nc.tensor.matmul(warm_bank[:, 0:P], lhsT=ident[:], rhs=ident[:], start=True, stop=True)
+        def next_bank(shape):
+            banks_taken.append(shape)
+            return psum.tile(shape, F32, name="bank%d" % (len(banks_taken) % PSUM_BANKS))
 
         c_rows = c_bytes.rearrange("(p i) k -> p i k", i=TOKEN_TILES)
         raw = {}
 
-        c_scale_sb = keep.tile([P, TOKEN_TILES * BLOCKS], F32, name="c_scale_sb")
-        nc.sync.dma_start(out=c_scale_sb[:], in_=c_scale.rearrange("(p i) j -> p (i j)", i=TOKEN_TILES))
-
-        def load_pair(r):
+        def load_passes(r, g0, g1):
+            k_cols = slice(g0 * K_PASS, g1 * K_PASS)
             if r < C_PAIRS:
-                rows = keep.tile([P, PAIR, K], U8, name="c_raw%d" % r)
-                src = c_rows[:, PAIR * r : PAIR * (r + 1), :]
+                src = c_rows[:, PAIR * r : PAIR * (r + 1), k_cols]
             else:
-                rows = keep.tile([P, PAIR, K], U8, name="w_raw%d" % r)
                 n0 = (r - C_PAIRS) * PAIR_ROWS
-                src = w_bytes[n0 : n0 + PAIR_ROWS, :].rearrange("(a p) k -> p a k", p=P)
+                src = w_bytes[n0 : n0 + PAIR_ROWS, k_cols].rearrange("(a p) k -> p a k", p=P)
+            rows = sbuf.tile([P, PAIR, (g1 - g0) * K_PASS], U8, name="raw%d_%d" % (r, g0))
             nc.sync.dma_start(out=rows[:], in_=src)
             for a in range(PAIR):
-                for g in range(PASSES):
-                    raw[(r, a, g)] = rows[:, a, g * K_PASS : (g + 1) * K_PASS]
+                for g in range(g0, g1):
+                    raw[(r, a, g)] = rows[:, a, (g - g0) * K_PASS : (g - g0 + 1) * K_PASS]
 
         v_codes = []
 
         def load_v_half(h):
-            words = keep.tile([P, PASSES, 2 * BANK], U8, name="v_codes%d" % h, align_bytes=64)
+            words = sbuf.tile([P, PASSES, 2 * BANK], U8, name="v_codes%d" % h, align_bytes=64)
             src = v_words.rearrange("g p n -> p g n")[:, :, 2 * BANK * h : 2 * BANK * (h + 1)]
             nc.sync.dma_start(out=words[:].bitcast(I32), in_=src.bitcast(I32))
             v_codes.append(words)
 
-        for g0, g1 in ((0, 1), (1, PASSES)):
-            piece = keep.tile([P, PAIR, (g1 - g0) * K_PASS], U8, name="c_raw_first%d" % g0)
-            nc.sync.dma_start(out=piece[:], in_=c_rows[:, 0:PAIR, g0 * K_PASS : g1 * K_PASS])
-            for a in range(PAIR):
-                for g in range(g0, g1):
-                    raw[(0, a, g)] = piece[:, a, (g - g0) * K_PASS : (g - g0 + 1) * K_PASS]
-        load_pair(1)
+        c_scale_sb = sbuf.tile([P, TOKEN_TILES * SCALE_COLS], F32, name="c_scale_sb")
+        nc.sync.dma_start(out=c_scale_sb[:], in_=c_scale.rearrange("(p i) j -> p (i j)", i=TOKEN_TILES))
+        load_passes(0, 0, 1)
+        load_passes(0, 1, PASSES)
+        load_passes(1, 0, PASSES)
         load_v_half(0)
-        v_plane_3d = v_plane[:].rearrange("p (g n) -> p g n", g=PASSES)
         for quad in range(4):
             nc.sync.dma_start(
-                out=v_plane_3d[32 * quad : 32 * quad + 4, :, :].bitcast(I32),
+                out=v_plane[:].rearrange("p (g n) -> p g n", g=PASSES)[32 * quad : 32 * quad + 4, :, :].bitcast(I32),
                 in_=v_scales.rearrange("g q n -> q g n")[4 * quad : 4 * quad + 4, :, :].bitcast(I32),
             )
         load_v_half(1)
-        load_pair(2)
-        gain_bf = keep.tile([P, TOKEN_TILES * HEADS], BF16, name="gain_bf")
+        load_passes(2, 0, PASSES)
+        gain_bf = sbuf.tile([P, TOKEN_TILES * HEADS], BF16, name="gain_bf")
         nc.sync.dma_start(out=gain_bf[:], in_=head_gain.rearrange("(p i) h -> p (i h)", i=TOKEN_TILES))
-        gain = keep.tile([P, TOKEN_TILES * HEADS], F32, name="gain")
+        gain = sbuf.tile([P, TOKEN_TILES * HEADS], F32, name="gain")
         nc.gpsimd.tensor_copy(out=gain[:], in_=gain_bf[:])
-        for r in range(3, C_PAIRS):
-            load_pair(r)
-        w_scale_sb = keep.tile([P, (NQ // B) * BLOCKS], F32, name="w_scale_sb")
+        load_passes(3, 0, PASSES)
+        w_scale_sb = sbuf.tile([P, (NQ // B) * SCALE_COLS], F32, name="w_scale_sb")
         nc.sync.dma_start(out=w_scale_sb[:], in_=w_scale.rearrange("a j -> (a j)").partition_broadcast(P))
         for r in range(C_PAIRS, PAIRS):
-            load_pair(r)
-        bias_sb = keep.tile([P, NQ], BF16, name="bias_sb")
+            load_passes(r, 0, PASSES)
+        bias_sb = sbuf.tile([P, NQ], BF16, name="bias_sb")
         nc.sync.dma_start(out=bias_sb[:], in_=bias.partition_broadcast(P))
 
         wide = {}
         flat = {}
-        grouped = {}
+        turned = {}
         codes = {}
         planes = {}
 
-        def on_scalar(r, a, g):
-            return a == 1 and (g < 2 if r < 2 else r >= C_PAIRS + 2 and g < 2 + r % 2)
-
         def widen(r, a, g):
-            dst = keep.tile(
-                [P, K_PASS], BF16, name="wide%d" % (((r * PASSES + g) * PAIR + a) % WIDE_RING), align_bytes=64
-            )
-            split = dst[:].rearrange("p (u m e) -> p m u e", u=2, e=2)
+            dst = sbuf.tile([P, K_PASS], BF16, name="wide%d" % (((r * PASSES + g) * PAIR + a) % WIDE_RING), align_bytes=64)
+            wide[(r, a, g)] = dst
+            halves = dst[:].rearrange("p (u m e) -> p m u e", u=2, e=2)
+            plain = dst
             if on_scalar(r, a, g) and r >= C_PAIRS:
-                flat[(r, g)] = keep.tile([P, K_PASS], BF16, name="flat%d" % g, align_bytes=64)
-            plain = flat.get((r, g), dst)
-            for q in range(BLOCKS_PER_PASS):
-                j = g * BLOCKS_PER_PASS + q
-                if r < C_PAIRS:
-                    col = (PAIR * r + a) * BLOCKS + j
-                    scale = c_scale_sb[:, col : col + 1]
-                else:
-                    col = (PAIR * (r - C_PAIRS) + a) * BLOCKS + j
-                    scale = w_scale_sb[:, col : col + 1]
+                plain = sbuf.tile([P, K_PASS], BF16, name="flat%d" % (len(flat) % FLAT_RING), align_bytes=64)
+                flat[(r, g)] = plain
+            scales, row_tile = (c_scale_sb, PAIR * r + a) if r < C_PAIRS else (w_scale_sb, PAIR * (r - C_PAIRS) + a)
+            for q in range(SCALES_PER_PASS):
+                col = row_tile * SCALE_COLS + g * SCALES_PER_PASS + q
                 src = raw[(r, a, g)][:, q * B : (q + 1) * B].bitcast(FP8)
                 if on_scalar(r, a, g):
-                    nc.scalar.activation(out=plain[:, q * B : (q + 1) * B], in_=src, func=COPY, scale=scale)
+                    nc.scalar.activation(
+                        out=plain[:, q * B : (q + 1) * B], in_=src, func=COPY, scale=scales[:, col : col + 1]
+                    )
                 else:
                     nc.vector.tensor_scalar(
-                        out=split[:, 32 * q : 32 * (q + 1), :, :],
+                        out=halves[:, q * B // PACK : (q + 1) * B // PACK, :, :],
                         in0=src.rearrange("p (m u e) -> p m u e", u=2, e=2),
-                        scalar1=scale,
+                        scalar1=scales[:, col : col + 1],
                         scalar2=None,
                         op0=MULT,
                     )
-            wide[(r, a, g)] = dst
 
         def part_words(r, g):
-            if (r, g) in flat:
-                nc.scalar.copy(
-                    out=wide[(r, 1, g)][:].bitcast(F32).rearrange("p (u m) -> p u m", u=2),
-                    in_=flat[(r, g)][:].bitcast(F32).rearrange("p (m u) -> p u m", u=2),
-                )
-
-        def widen_pass(r, g):
-            if r < PAIRS:
-                for a in range(PAIR):
-                    widen(r, a, g)
+            nc.scalar.copy(
+                out=wide[(r, 1, g)][:].bitcast(F32).rearrange("p (u m) -> p u m", u=2),
+                in_=flat[(r, g)][:].bitcast(F32).rearrange("p (m u) -> p u m", u=2),
+            )
 
         def turn(r, g):
-            bank = psum.tile([P, PAIR, 2, P], F32, name="turn%d" % g)
+            bank = next_bank([P, PAIR, 2, P])
             for a in range(PAIR):
                 words = wide[(r, a, g)][:].bitcast(F32)
                 for u in range(2):
-                    half = words[:, u : 2 * P : 2] if on_scalar(r, a, g) and r < C_PAIRS else words[:, u * P : (u + 1) * P]
+                    plain_order = on_scalar(r, a, g) and r < C_PAIRS
+                    half = words[:, u : 2 * P : 2] if plain_order else words[:, u * P : (u + 1) * P]
                     nc.tensor.transpose(bank[:, a, u, :], half, ident[:])
-            dst = keep.tile(
-                [P, PAIR_ROWS * 4], BF16, name="grouped%d" % ((r * PASSES + g) % GROUPED_RING), align_bytes=64
-            )
+            if r < C_PAIRS:
+                group, place, size = r, 0, 1
+            else:
+                j, place = divmod(r - C_PAIRS, PAIRS_PER_CHUNK)
+                group, size = C_PAIRS + j, PAIRS_PER_CHUNK
+            width = PAIR_ROWS * PACK
+            if place == 0:
+                name = "turned%d" % (len(turned) % TURNED_RING)
+                turned[(group, g)] = sbuf.tile([P, size * width], BF16, name=name, align_bytes=64)
+            dst = turned[(group, g)][:, place * width : (place + 1) * width]
             nc.scalar.copy(
-                out=dst[:].bitcast(F32).rearrange("p (a r u) -> p a r u", a=PAIR, u=2),
+                out=dst.bitcast(F32).rearrange("p (a r u) -> p a r u", a=PAIR, u=2),
                 in_=bank[:].rearrange("p a u r -> p a r u"),
             )
-            grouped[(r, g)] = dst
 
-        def quantize(r, g):
-            words = keep.tile([P, PAIR_ROWS], U32, name="codes%d_%d" % (r, g), align_bytes=64)
-            plane = keep.tile([P, PAIR_ROWS], U8, name="plane%d_%d" % (r, g), align_bytes=64)
-            nc.vector.quantize_mx(out=words[:].bitcast(FP8X4), scales=plane[:], in_=grouped[(r, g)][:])
-            codes[(r, g)] = words
-            planes[(r, g)] = plane
+        def turn_pairs(pairs):
+            for g in range(PASSES):
+                for r in pairs:
+                    turn(r, g)
 
-        acc = {}
+        def quantize(group, g):
+            rows = turned[(group, g)].shape[1] // PACK
+            words = sbuf.tile([P, rows], U32, name="codes%d_%d" % (group, g), align_bytes=64)
+            plane = sbuf.tile([P, rows], U8, name="plane%d_%d" % (group, g), align_bytes=64)
+            nc.vector.quantize_mx(out=words[:].bitcast(FP8X4), scales=plane[:], in_=turned[(group, g)][:])
+            codes[(group, g)] = words
+            planes[(group, g)] = plane
+
+        sums = {}
         main_rows = out_0.rearrange("(p i) n -> p i n", i=TOKEN_TILES)
         index_rows = out_1.rearrange("(p i) n -> p i n", i=TOKEN_TILES)
 
-        def multiply(s, b, tiles=(0, 1)):
-            bank = psum.tile([P, BANK], F32, name="acc%d" % (len(acc) % ACC_BANKS))
-            if s < C_PAIRS:
-                a, h = divmod(b, 2)
-                for g in range(PASSES):
-                    nc.tensor.matmul_mx(
-                        out=bank[:],
-                        lhsT=codes[(s, g)][:, a * P : (a + 1) * P].bitcast(FP8X4),
-                        lhsT_scale=planes[(s, g)][:, a * P : (a + 1) * P],
-                        rhs=v_codes[h][:, g, :].bitcast(FP4X4),
-                        rhs_scale=v_plane[:, g * NI + h * BANK : g * NI + (h + 1) * BANK],
-                        start=(g == 0),
-                        stop=(g == PASSES - 1),
-                    )
-            else:
-                for a in tiles:
-                    for g in range(PASSES):
-                        nc.tensor.matmul_mx(
-                            out=bank[:, a * PAIR_ROWS : (a + 1) * PAIR_ROWS],
-                            lhsT=codes[(b, g)][:, a * P : (a + 1) * P].bitcast(FP8X4),
-                            lhsT_scale=planes[(b, g)][:, a * P : (a + 1) * P],
-                            rhs=codes[(s, g)][:].bitcast(FP8X4),
-                            rhs_scale=planes[(s, g)][:],
-                            start=(g == 0),
-                            stop=(g == PASSES - 1),
-                        )
-            acc[(s, b, tiles)] = (bank, len(acc))
+        def multiply(s, b, span=(0, BANK)):
+            cols = slice(*span)
+            bank = next_bank([P, BANK])
+            r, a = (s, b // 2) if s < C_PAIRS else divmod(b, PAIR)
+            tokens = slice(a * P, (a + 1) * P)
+            for g in range(PASSES):
+                if s < C_PAIRS:
+                    h = b % 2
+                    rhs = v_codes[h][:, g, :].bitcast(FP4X4)
+                    rhs_scale = v_plane[:, g * NI + h * BANK : g * NI + (h + 1) * BANK]
+                else:
+                    rhs = codes[(s, g)][:, cols].bitcast(FP8X4)
+                    rhs_scale = planes[(s, g)][:, cols]
+                nc.tensor.matmul_mx(
+                    out=bank[:, cols],
+                    lhsT=codes[(r, g)][:, tokens].bitcast(FP8X4),
+                    lhsT_scale=planes[(r, g)][:, tokens],
+                    rhs=rhs,
+                    rhs_scale=rhs_scale,
+                    start=(g == 0),
+                    stop=(g == PASSES - 1),
+                )
+            sums[(s, b, span)] = (bank, len(sums))
 
-        def finish(s, b, tiles=(0, 1)):
-            bank, number = acc[(s, b, tiles)]
-            stage = keep.tile([P, BANK], F32, name="stage%d" % (number % STAGE_RING))
+        def finish(s, b, span=(0, BANK)):
+            cols = slice(*span)
+            bank, number = sums[(s, b, span)]
+            stage = sbuf.tile([P, BANK], F32, name="stage%d" % (number % STAGE_RING))
             if s < C_PAIRS:
                 a, h = divmod(b, 2)
                 i = PAIR * s + a
-                heads = BANK // D
-                first = i * HEADS + h * heads
-                if b == BANKS_PER_STEP - 1:
+                first = i * HEADS + h * HEADS_PER_BANK
+                if b == INDEX_BANKS - 1:
                     nc.vector.tensor_tensor(
                         out=stage[:].rearrange("p (h d) -> p h d", d=D),
                         in0=bank[:].rearrange("p (h d) -> p h d", d=D),
-                        in1=gain[:, first : first + heads].unsqueeze(2).to_broadcast([P, heads, D]),
+                        in1=gain[:, first : first + HEADS_PER_BANK].unsqueeze(2).to_broadcast([P, HEADS_PER_BANK, D]),
                         op=MULT,
                     )
                 else:
-                    for e in range(heads):
+                    for e in range(HEADS_PER_BANK):
                         nc.scalar.activation(
                             out=stage[:, e * D : (e + 1) * D],
                             in_=bank[:, e * D : (e + 1) * D],
@@ -245,23 +261,23 @@ def tile_latent_query_up_projection_d6_kernel(
                         )
                 nc.sync.dma_start(out=index_rows[:, i, h * BANK : (h + 1) * BANK], in_=stage[:])
             else:
-                n0 = (s - C_PAIRS) * PAIR_ROWS
-                a0, a1 = tiles[0], tiles[-1] + 1
-                rows = stage[:].rearrange("p (a n) -> p a n", a=PAIR)[:, a0:a1, :]
-                nc.vector.tensor_tensor(
-                    out=rows,
-                    in0=bank[:].rearrange("p (a n) -> p a n", a=PAIR)[:, a0:a1, :],
-                    in1=bias_sb[:, n0 : n0 + PAIR_ROWS].unsqueeze(1).to_broadcast([P, a1 - a0, PAIR_ROWS]),
-                    op=ADD,
-                )
-                nc.sync.dma_start(out=main_rows[:, PAIR * b + a0 : PAIR * b + a1, n0 : n0 + PAIR_ROWS], in_=rows)
+                n0 = (s - C_PAIRS) * BANK
+                outs = slice(n0 + span[0], n0 + span[1])
+                nc.vector.tensor_tensor(out=stage[:, cols], in0=bank[:, cols], in1=bias_sb[:, outs], op=ADD)
+                nc.sync.dma_start(out=main_rows[:, b, outs], in_=stage[:, cols])
 
-        warm_up(4)
+        warm_bank = next_bank([P, P])
+
+        def warm_up(count):
+            for n in range(count):
+                nc.tensor.matmul(warm_bank[:], lhsT=ident[:], rhs=ident[:], start=True, stop=True)
+
+        warm_up(WARM_FIRST)
         for g in range(PASSES):
-            widen_pass(0, g)
-        for g in range(PASSES):
-            turn(0, g)
-        warm_up(2)
+            for a in range(PAIR):
+                widen(0, a, g)
+        turn_pairs([0])
+        warm_up(WARM_SECOND)
         quantize(0, 0)
         widen(1, 0, 0)
         quantize(0, 1)
@@ -271,56 +287,73 @@ def tile_latent_query_up_projection_d6_kernel(
         for g in range(PASSES):
             widen(1, 1, g)
         multiply(0, 0)
-        for g in range(PASSES):
-            turn(1, g)
+        turn_pairs([1])
         multiply(0, 1)
-        widen_pass(2, 0)
-        widen_pass(2, 1)
-        quantize(1, 0)
-        widen(2, 0, 2)
-        quantize(1, 1)
-        widen(2, 1, 2)
-        quantize(1, 2)
+
+        todo = [(r, a, g) for r in range(2, PAIRS) for g in range(PASSES) for a in range(PAIR) if not on_scalar(r, a, g)]
+
+        def widen_next(count):
+            for unit in todo[:count]:
+                widen(*unit)
+                todo.remove(unit)
+
+        widen_next(4)
+        for g in range(PASSES):
+            quantize(1, g)
+            if g + 1 < PASSES:
+                widen_next(1)
         multiply(0, 2)
         multiply(0, 3)
-        for b in range(3):
+        for b in range(INDEX_BANKS - 1):
             finish(0, b)
 
-        for s in range(1, PAIRS):
-            ahead = s + 1 < PAIRS
-            later = s + 2 < PAIRS
-            if ahead:
-                for g in range(PASSES):
-                    turn(s + 1, g)
-            finish(s - 1, BANKS_PER_STEP - 1)
-            if later:
-                widen(s + 2, 0, 0)
-            if ahead:
-                quantize(s + 1, 0)
-            if later:
-                widen(s + 2, 0, 1)
-            if ahead:
-                quantize(s + 1, 1)
-            if later:
-                widen(s + 2, 1, 0)
-            multiply(s, 0)
-            finish(s, 0)
-            if ahead:
-                quantize(s + 1, 2)
-            if later:
-                widen(s + 2, 0, 2)
-                widen(s + 2, 1, 1)
-                part_words(s + 2, 0)
-            multiply(s, 1)
-            finish(s, 1)
-            if later:
-                widen(s + 2, 1, 2)
-                part_words(s + 2, 1)
-                part_words(s + 2, 2)
-            multiply(s, 2)
-            finish(s, 2)
-            if ahead:
-                multiply(s, 3)
-        for a in range(PAIR):
-            multiply(PAIRS - 1, BANKS_PER_STEP - 1, (a,))
-            finish(PAIRS - 1, BANKS_PER_STEP - 1, (a,))
+        for s in range(1, C_PAIRS):
+            last = s == C_PAIRS - 1
+            turn_pairs(chunk_pairs(0) if last else [s + 1])
+            finish(s - 1, INDEX_BANKS - 1)
+            widen_next(3 if last else 1)
+            for g in range(PASSES):
+                quantize(s + 1, g)
+                if g + 1 < PASSES:
+                    widen_next(1)
+            widen_next(3 if last else WIDEN_PER_C_STEP - PASSES)
+            for b in range(INDEX_BANKS):
+                multiply(s, b)
+                if b + 1 < INDEX_BANKS:
+                    finish(s, b)
+
+        def scalar_share(j):
+            units = [(r, g) for g in range(PASSES) for r in chunk_pairs(j) if on_scalar(r, 1, g)]
+            for n, (r, g) in enumerate(units):
+                widen(r, 1, g)
+                if n > 0:
+                    part_words(*units[n - 1])
+            part_words(*units[-1])
+
+        scalar_share(1)
+        waiting = (C_PAIRS - 1, INDEX_BANKS - 1)
+        for j in range(CHUNKS):
+            s = C_PAIRS + j
+            ahead = j + 1 < CHUNKS
+            for i in range(TOKEN_TILES):
+                if ahead and i == TURN_AT:
+                    turn_pairs(chunk_pairs(j + 1))
+                    if j + 2 < CHUNKS:
+                        scalar_share(j + 2)
+                finish(*waiting)
+                if ahead and i == TURN_AT:
+                    widen_next(2)
+                    quantize(s + 1, 0)
+                    widen_next(1)
+                    quantize(s + 1, 1)
+                elif ahead and i == TURN_AT + 1:
+                    quantize(s + 1, 2)
+                elif i < TURN_AT:
+                    widen_next(1)
+                if ahead or i + 1 < TOKEN_TILES:
+                    multiply(s, i)
+                    waiting = (s, i)
+
+        for span in ((0, BANK // 2), (BANK // 2, BANK)):
+            multiply(C_PAIRS + CHUNKS - 1, TOKEN_TILES - 1, span)
+            finish(C_PAIRS + CHUNKS - 1, TOKEN_TILES - 1, span)

@@ -42,7 +42,6 @@ FLAT_RING = 4
 TURNED_RING = 4
 STAGE_RING = 20
 
-WARM_FIRST, WARM_SECOND = 4, 2
 WIDEN_PER_C_STEP = 9
 TURN_AT = TOKEN_TILES // 2
 
@@ -266,18 +265,10 @@ def tile_latent_query_up_projection_d6_kernel(
                 nc.vector.tensor_tensor(out=stage[:, cols], in0=bank[:, cols], in1=bias_sb[:, outs], op=ADD)
                 nc.sync.dma_start(out=main_rows[:, b, outs], in_=stage[:, cols])
 
-        warm_bank = next_bank([P, P])
-
-        def warm_up(count):
-            for n in range(count):
-                nc.tensor.matmul(warm_bank[:], lhsT=ident[:], rhs=ident[:], start=True, stop=True)
-
-        warm_up(WARM_FIRST)
         for g in range(PASSES):
             for a in range(PAIR):
                 widen(0, a, g)
         turn_pairs([0])
-        warm_up(WARM_SECOND)
         quantize(0, 0)
         widen(1, 0, 0)
         quantize(0, 1)

from contextlib import ExitStack

import concourse.mybir as mybir
from concourse.masks import make_identity

T, K, NQ, NI, D, B = 1024, 1536, 2048, 1024, 128, 128
FLOPS = 2 * T * K * (NQ + NI)

F32 = mybir.dt.float32
BF16 = mybir.dt.bfloat16
I32 = mybir.dt.int32
U32 = mybir.dt.uint32
U8 = mybir.dt.uint8
FP8 = mybir.dt.float8_e4m3fn
FP8X4 = mybir.dt.float8_e4m3fn_x4
FP4X4 = mybir.dt.float4_e2m1fn_x4
MULT = mybir.AluOpType.mult
ADD = mybir.AluOpType.add
COPY = mybir.ActivationFunctionType.Copy

P = 128
PACK = 4
K_PASS = P * PACK
PASSES = K // K_PASS
SCALE_COLS = K // B
SCALES_PER_PASS = K_PASS // B
TOKEN_TILES = T // P
HEADS = NI // D
BANK = 512
HEADS_PER_BANK = BANK // D
PAIR = 2
PAIR_ROWS = PAIR * P
C_PAIRS = T // PAIR_ROWS
PAIRS = C_PAIRS + NQ // PAIR_ROWS
CHUNKS = NQ // BANK
PAIRS_PER_CHUNK = BANK // PAIR_ROWS
INDEX_BANKS = PAIR * NI // BANK

PSUM_BANKS = 8
WIDE_RING = 24
FLAT_RING = 4
TURNED_RING = 4
STAGE_RING = 20

WIDEN_PER_C_STEP = 9
TURN_AT = TOKEN_TILES // 2


def scalar_passes(r):
    if r < 2:
        return 2
    if r < C_PAIRS + PAIRS_PER_CHUNK:
        return 0
    if r < C_PAIRS + 2 * PAIRS_PER_CHUNK:
        return 1
    return 2 + r % 2


def on_scalar(r, a, g):
    return a == 1 and g < scalar_passes(r)


def chunk_pairs(j):
    return range(C_PAIRS + PAIRS_PER_CHUNK * j, C_PAIRS + PAIRS_PER_CHUNK * (j + 1))


def tile_latent_query_up_projection_d6_kernel(
    tc, c_bytes, c_scale, w_bytes, w_scale, v_words, v_scales, bias, head_gain, out_0, out_1
):
    nc = tc.nc
    with ExitStack() as ctx:
        sbuf = ctx.enter_context(tc.tile_pool(name="sbuf", bufs=1))
        psum = ctx.enter_context(tc.psum_pool(name="psum", bufs=1))
        ctx.enter_context(tc.manual_schedule())

        ident = sbuf.tile([P, P], F32, name="ident")
        make_identity(nc, ident[:])

        v_plane = sbuf.tile([P, PASSES * NI], U8, name="v_plane", align_bytes=64)
        nc.vector.memset(v_plane[:].bitcast(I32), 0)

        banks_taken = []

        def next_bank(shape):
            banks_taken.append(shape)
            return psum.tile(shape, F32, name="bank%d" % (len(banks_taken) % PSUM_BANKS))

        c_rows = c_bytes.rearrange("(p i) k -> p i k", i=TOKEN_TILES)
        raw = {}

        def load_passes(r, g0, g1):
            k_cols = slice(g0 * K_PASS, g1 * K_PASS)
            if r < C_PAIRS:
                src = c_rows[:, PAIR * r : PAIR * (r + 1), k_cols]
            else:
                n0 = (r - C_PAIRS) * PAIR_ROWS
                src = w_bytes[n0 : n0 + PAIR_ROWS, k_cols].rearrange("(a p) k -> p a k", p=P)
            rows = sbuf.tile([P, PAIR, (g1 - g0) * K_PASS], U8, name="raw%d_%d" % (r, g0))
            nc.sync.dma_start(out=rows[:], in_=src)
            for a in range(PAIR):
                for g in range(g0, g1):
                    raw[(r, a, g)] = rows[:, a, (g - g0) * K_PASS : (g - g0 + 1) * K_PASS]

        v_codes = []

        def load_v_half(h):
            words = sbuf.tile([P, PASSES, 2 * BANK], U8, name="v_codes%d" % h, align_bytes=64)
            src = v_words.rearrange("g p n -> p g n")[:, :, 2 * BANK * h : 2 * BANK * (h + 1)]
            nc.sync.dma_start(out=words[:].bitcast(I32), in_=src.bitcast(I32))
            v_codes.append(words)

        c_scale_sb = sbuf.tile([P, TOKEN_TILES * SCALE_COLS], F32, name="c_scale_sb")
        nc.sync.dma_start(out=c_scale_sb[:], in_=c_scale.rearrange("(p i) j -> p (i j)", i=TOKEN_TILES))
        load_passes(0, 0, 1)
        load_passes(0, 1, PASSES)
        load_passes(1, 0, PASSES)
        load_v_half(0)
        for quad in range(4):
            nc.sync.dma_start(
                out=v_plane[:].rearrange("p (g n) -> p g n", g=PASSES)[32 * quad : 32 * quad + 4, :, :].bitcast(I32),
                in_=v_scales.rearrange("g q n -> q g n")[4 * quad : 4 * quad + 4, :, :].bitcast(I32),
            )
        load_v_half(1)
        load_passes(2, 0, PASSES)
        gain_bf = sbuf.tile([P, TOKEN_TILES * HEADS], BF16, name="gain_bf")
        nc.sync.dma_start(out=gain_bf[:], in_=head_gain.rearrange("(p i) h -> p (i h)", i=TOKEN_TILES))
        gain = sbuf.tile([P, TOKEN_TILES * HEADS], F32, name="gain")
        nc.gpsimd.tensor_copy(out=gain[:], in_=gain_bf[:])
        load_passes(3, 0, PASSES)
        w_scale_sb = sbuf.tile([P, (NQ // B) * SCALE_COLS], F32, name="w_scale_sb")
        nc.sync.dma_start(out=w_scale_sb[:], in_=w_scale.rearrange("a j -> (a j)").partition_broadcast(P))
        for r in range(C_PAIRS, PAIRS):
            load_passes(r, 0, PASSES)
        bias_sb = sbuf.tile([P, NQ], BF16, name="bias_sb")
        nc.sync.dma_start(out=bias_sb[:], in_=bias.partition_broadcast(P))

        wide = {}
        flat = {}
        turned = {}
        codes = {}
        planes = {}

        def widen(r, a, g):
            dst = sbuf.tile([P, K_PASS], BF16, name="wide%d" % (((r * PASSES + g) * PAIR + a) % WIDE_RING), align_bytes=64)
            wide[(r, a, g)] = dst
            halves = dst[:].rearrange("p (u m e) -> p m u e", u=2, e=2)
            plain = dst
            if on_scalar(r, a, g) and r >= C_PAIRS:
                plain = sbuf.tile([P, K_PASS], BF16, name="flat%d" % (len(flat) % FLAT_RING), align_bytes=64)
                flat[(r, g)] = plain
            scales, row_tile = (c_scale_sb, PAIR * r + a) if r < C_PAIRS else (w_scale_sb, PAIR * (r - C_PAIRS) + a)
            for q in range(SCALES_PER_PASS):
                col = row_tile * SCALE_COLS + g * SCALES_PER_PASS + q
                src = raw[(r, a, g)][:, q * B : (q + 1) * B].bitcast(FP8)
                if on_scalar(r, a, g):
                    nc.scalar.activation(
                        out=plain[:, q * B : (q + 1) * B], in_=src, func=COPY, scale=scales[:, col : col + 1]
                    )
                else:
                    nc.vector.tensor_scalar(
                        out=halves[:, q * B // PACK : (q + 1) * B // PACK, :, :],
                        in0=src.rearrange("p (m u e) -> p m u e", u=2, e=2),
                        scalar1=scales[:, col : col + 1],
                        scalar2=None,
                        op0=MULT,
                    )

        def part_words(r, g):
            nc.scalar.copy(
                out=wide[(r, 1, g)][:].bitcast(F32).rearrange("p (u m) -> p u m", u=2),
                in_=flat[(r, g)][:].bitcast(F32).rearrange("p (m u) -> p u m", u=2),
            )

        def turn(r, g):
            bank = next_bank([P, PAIR, 2, P])
            for a in range(PAIR):
                words = wide[(r, a, g)][:].bitcast(F32)
                for u in range(2):
                    plain_order = on_scalar(r, a, g) and r < C_PAIRS
                    half = words[:, u : 2 * P : 2] if plain_order else words[:, u * P : (u + 1) * P]
                    nc.tensor.transpose(bank[:, a, u, :], half, ident[:])
            if r < C_PAIRS:
                group, place, size = r, 0, 1
            else:
                j, place = divmod(r - C_PAIRS, PAIRS_PER_CHUNK)
                group, size = C_PAIRS + j, PAIRS_PER_CHUNK
            width = PAIR_ROWS * PACK
            if place == 0:
                name = "turned%d" % (len(turned) % TURNED_RING)
                turned[(group, g)] = sbuf.tile([P, size * width], BF16, name=name, align_bytes=64)
            dst = turned[(group, g)][:, place * width : (place + 1) * width]
            nc.scalar.copy(
                out=dst.bitcast(F32).rearrange("p (a r u) -> p a r u", a=PAIR, u=2),
                in_=bank[:].rearrange("p a u r -> p a r u"),
            )

        def turn_pairs(pairs):
            for g in range(PASSES):
                for r in pairs:
                    turn(r, g)

        def quantize(group, g):
            rows = turned[(group, g)].shape[1] // PACK
            words = sbuf.tile([P, rows], U32, name="codes%d_%d" % (group, g), align_bytes=64)
            plane = sbuf.tile([P, rows], U8, name="plane%d_%d" % (group, g), align_bytes=64)
            nc.vector.quantize_mx(out=words[:].bitcast(FP8X4), scales=plane[:], in_=turned[(group, g)][:])
            codes[(group, g)] = words
            planes[(group, g)] = plane

        sums = {}
        main_rows = out_0.rearrange("(p i) n -> p i n", i=TOKEN_TILES)
        index_rows = out_1.rearrange("(p i) n -> p i n", i=TOKEN_TILES)

        def multiply(s, b, span=(0, BANK)):
            cols = slice(*span)
            bank = next_bank([P, BANK])
            r, a = (s, b // 2) if s < C_PAIRS else divmod(b, PAIR)
            tokens = slice(a * P, (a + 1) * P)
            for g in range(PASSES):
                if s < C_PAIRS:
                    h = b % 2
                    rhs = v_codes[h][:, g, :].bitcast(FP4X4)
                    rhs_scale = v_plane[:, g * NI + h * BANK : g * NI + (h + 1) * BANK]
                else:
                    rhs = codes[(s, g)][:, cols].bitcast(FP8X4)
                    rhs_scale = planes[(s, g)][:, cols]
                nc.tensor.matmul_mx(
                    out=bank[:, cols],
                    lhsT=codes[(r, g)][:, tokens].bitcast(FP8X4),
                    lhsT_scale=planes[(r, g)][:, tokens],
                    rhs=rhs,
                    rhs_scale=rhs_scale,
                    start=(g == 0),
                    stop=(g == PASSES - 1),
                )
            sums[(s, b, span)] = (bank, len(sums))

        def finish(s, b, span=(0, BANK)):
            cols = slice(*span)
            bank, number = sums[(s, b, span)]
            stage = sbuf.tile([P, BANK], F32, name="stage%d" % (number % STAGE_RING))
            if s < C_PAIRS:
                a, h = divmod(b, 2)
                i = PAIR * s + a
                first = i * HEADS + h * HEADS_PER_BANK
                if b == INDEX_BANKS - 1:
                    nc.vector.tensor_tensor(
                        out=stage[:].rearrange("p (h d) -> p h d", d=D),
                        in0=bank[:].rearrange("p (h d) -> p h d", d=D),
                        in1=gain[:, first : first + HEADS_PER_BANK].unsqueeze(2).to_broadcast([P, HEADS_PER_BANK, D]),
                        op=MULT,
                    )
                else:
                    for e in range(HEADS_PER_BANK):
                        nc.scalar.activation(
                            out=stage[:, e * D : (e + 1) * D],
                            in_=bank[:, e * D : (e + 1) * D],
                            func=COPY,
                            scale=gain[:, first + e : first + e + 1],
                        )
                nc.sync.dma_start(out=index_rows[:, i, h * BANK : (h + 1) * BANK], in_=stage[:])
            else:
                n0 = (s - C_PAIRS) * BANK
                outs = slice(n0 + span[0], n0 + span[1])
                nc.vector.tensor_tensor(out=stage[:, cols], in0=bank[:, cols], in1=bias_sb[:, outs], op=ADD)
                nc.sync.dma_start(out=main_rows[:, b, outs], in_=stage[:, cols])

        for g in range(PASSES):
            for a in range(PAIR):
                widen(0, a, g)
        turn_pairs([0])
        quantize(0, 0)
        widen(1, 0, 0)
        quantize(0, 1)
        quantize(0, 2)
        widen(1, 0, 1)
        widen(1, 0, 2)
        for g in range(PASSES):
            widen(1, 1, g)
        multiply(0, 0)
        turn_pairs([1])
        multiply(0, 1)

        todo = [(r, a, g) for r in range(2, PAIRS) for g in range(PASSES) for a in range(PAIR) if not on_scalar(r, a, g)]

        def widen_next(count):
            for unit in todo[:count]:
                widen(*unit)
                todo.remove(unit)

        widen_next(4)
        for g in range(PASSES):
            quantize(1, g)
            if g + 1 < PASSES:
                widen_next(1)
        multiply(0, 2)
        multiply(0, 3)
        for b in range(INDEX_BANKS - 1):
            finish(0, b)

        for s in range(1, C_PAIRS):
            last = s == C_PAIRS - 1
            turn_pairs(chunk_pairs(0) if last else [s + 1])
            finish(s - 1, INDEX_BANKS - 1)
            widen_next(3 if last else 1)
            for g in range(PASSES):
                quantize(s + 1, g)
                if g + 1 < PASSES:
                    widen_next(1)
            widen_next(3 if last else WIDEN_PER_C_STEP - PASSES)
            for b in range(INDEX_BANKS):
                multiply(s, b)
                if b + 1 < INDEX_BANKS:
                    finish(s, b)

        def scalar_share(j):
            units = [(r, g) for g in range(PASSES) for r in chunk_pairs(j) if on_scalar(r, 1, g)]
            for n, (r, g) in enumerate(units):
                widen(r, 1, g)
                if n > 0:
                    part_words(*units[n - 1])
            part_words(*units[-1])

        scalar_share(1)
        waiting = (C_PAIRS - 1, INDEX_BANKS - 1)
        for j in range(CHUNKS):
            s = C_PAIRS + j
            ahead = j + 1 < CHUNKS
            for i in range(TOKEN_TILES):
                if ahead and i == TURN_AT:
                    turn_pairs(chunk_pairs(j + 1))
                    if j + 2 < CHUNKS:
                        scalar_share(j + 2)
                finish(*waiting)
                if ahead and i == TURN_AT:
                    widen_next(2)
                    quantize(s + 1, 0)
                    widen_next(1)
                    quantize(s + 1, 1)
                elif ahead and i == TURN_AT + 1:
                    quantize(s + 1, 2)
                elif i < TURN_AT:
                    widen_next(1)
                if ahead or i + 1 < TOKEN_TILES:
                    multiply(s, i)
                    waiting = (s, i)

        for span in ((0, BANK // 2), (BANK // 2, BANK)):
            multiply(C_PAIRS + CHUNKS - 1, TOKEN_TILES - 1, span)
            finish(C_PAIRS + CHUNKS - 1, TOKEN_TILES - 1, span)
